import numpy as np
CORES = [0,4,8,12,16,20,24,28,32,36,40,44,48,52,56,60,64,68,72,76,80,84,88,92,96,100,104,108,112,116,120,124]
N = 32
def setup_inputs(rng):
    return {"x": rng.standard_normal((N, 128, 32), dtype=np.float32)}
def reference(x):
    b = 32 // N
    blocks = x.reshape(N, 128, N, b)
    return {"y": np.ascontiguousarray(blocks.transpose(2, 1, 0, 3)).reshape(N, 128, 32)}

import concourse.bass as bass

SCRATCH = {
    "xs": ("sbuf", [128, 32], "float32"),
    "hx": ("sbuf", [128, 16], "float32"),
    "land": ("sbuf", [128, 32], "float32"),
}
SEMAPHORES = ["local", "sent", "arrived"]

ON_CHIP_A = 0x0F00
ON_CHIP_B = 0xF000


def rank_program(g, core, T, topo):
    chip, k = divmod(core, 8)
    half, role = divmod(k, 4)
    r = 2 * chip + half
    own = chip // 8
    parity = chip & 1

    def dst_id(c):
        rid, pid, _se = topo.addr(c)
        return bass.DstId(rid=rid, pnc=pid)

    def columns(src, base, dests):
        transfers, engines, off, on = [], 0, 0, [ON_CHIP_A, ON_CHIP_B]
        for d in dests:
            c = T.cores[d]
            if topo.chip(c) == chip:
                m, n = on.pop(0), 4
            else:
                m, n = 1 << off, 1
                off += 1
            engines += n
            transfers.append(bass.RemoteDMATransfer(
                dst_ids=[dst_id(c)], dma_engine_mask=m, remote_sem=T.sem.arrived,
                src=src[:, d - base:d - base + 1], dst=T.land[:, r:r + 1]))
        g.remote_dma_fused(transfers, local_sem=T.sem.sent)
        return engines

    def in_half(h, par):
        return [d for d in range(16 * h, 16 * h + 16) if ((d // 2) & 1) == par]

    if role == 0:
        g.dma_start(T.xs[:], T.x[:]).then_inc(T.sem.local, 16)
        g.wait_ge(T.sem.local, 16)
        transfers = []
        for h in (0, 1):
            to = [core + 2 + h] + ([core + 1] if h == own else [])
            transfers.append(bass.RemoteDMATransfer(
                dst_ids=[dst_id(c) for c in to], dma_engine_mask=0x00FF << (8 * h), remote_sem=T.sem.arrived,
                srcs=[T.xs[:, 16 * h:16 * h + 16]], dsts=[T.hx[:] for c in to]))
        g.remote_dma_fused(transfers, local_sem=T.sem.sent)
        n = 16 + columns(T.xs, 0, in_half(1 - own, parity))
        g.wait_ge(T.sem.arrived, 30 + 4 + 4)
        g.dma_start(T.y[:], T.land[:]).then_inc(T.sem.local, 16)
        g.wait_ge(T.sem.sent, n)
        g.wait_ge(T.sem.local, 32)
        return

    g.wait_ge(T.sem.arrived, 8)
    if role == 1:
        n = columns(T.hx, 16 * own, in_half(own, parity))
    else:
        n = columns(T.hx, 16 * (role - 2), in_half(role - 2, 1 - parity))
    g.wait_ge(T.sem.sent, n)
